import numpy as np
import ml_dtypes


def mxq(x, axis, fmt="e4m3"):
    dtype, down = {"e4m3": (ml_dtypes.float8_e4m3fn, 7), "e5m2": (ml_dtypes.float8_e5m2, 14)}[fmt]
    v = np.moveaxis(np.asarray(x, np.float32).astype(ml_dtypes.bfloat16).astype(np.float64), axis, -1)
    blocks = v.reshape(v.shape[:-1] + (-1, 32))
    amax = np.abs(blocks).max(-1, keepdims=True)
    byte = np.maximum(np.where(amax > 0, np.frexp(amax)[1] - 1 + 127, 0) - down, 1)
    scale = np.exp2(byte - 127.0)
    codes = (blocks / scale).astype(np.float32).astype(dtype).astype(np.float64)
    return np.moveaxis((codes * scale).reshape(v.shape), -1, axis)


WIDE = False


def mx_kscale(k):
    if not WIDE:
        return np.ones(k)
    levels = np.array([10, -10, 5, -5, 0])
    if k % 512:
        return np.exp2(np.random.permutation(np.resize(levels, k // 32))).repeat(32)
    a = np.empty((k // 512, 16))
    for p in range(k // 512):
        a[p, :8] = np.random.permutation(np.resize(levels, 8))
        for g in range(8):
            far = levels[np.abs(levels - a[p, g]) >= 10]
            a[p, g + 8] = far[np.random.randint(len(far))]
    return np.exp2(a.ravel()).repeat(32)


def f64(x):
    return np.asarray(x).astype(np.float64)


def striped(idx):
    return np.tile(idx.reshape(-1, 16).T, (8, 1)).astype(np.uint16)


def unstriped(offs):
    return offs[:16].T.reshape(-1).astype(np.int64)


def pack_weight(w):
    k, n = w.shape
    w = f64(np.asarray(w, np.float32).astype(ml_dtypes.bfloat16)).reshape(k // 32, 32, n)
    amax = np.abs(w).max(1)
    byte = np.clip(np.where(amax > 0, np.frexp(amax)[1] - 1 + 127 - 7, 1), 1, 254)
    scaled = (w * np.exp2(127.0 - byte)[:, None, :]).reshape(k, n).astype(np.float32)
    words = np.ascontiguousarray(scaled.reshape(k // 512, 128, 4, n).transpose(0, 1, 3, 2)).astype(ml_dtypes.float8_e4m3fn).view(np.uint8)
    return words, np.ascontiguousarray(byte.astype(np.uint8).reshape(k // 512, 16, n))


def unpack_weight(words, scales):
    g, p, n, _ = words.shape
    vals = np.ascontiguousarray(words).view(ml_dtypes.float8_e4m3fn).astype(np.float64) * np.repeat(np.exp2(scales.astype(np.float64) - 127.0), 8, axis=1)[..., None]
    return vals.transpose(0, 1, 3, 2).reshape(g * 512, n)


K, T, S, D, N, V = 1024, 1024, 512, 2, 128, 256


def setup_inputs():
    n = np.random.standard_normal
    s = mx_kscale(K)[:, None]
    packed_xT = pack_weight(n((K, T)) * s)
    return {
        "x_words": packed_xT[0],
        "x_scales": packed_xT[1],
        "w1": (n((K, N)) / np.sqrt(K) / s).astype(np.float32),
        "val0": (-np.random.uniform(0.0, 3.0, (N, V))).astype(np.float32),
        "offs": striped(np.random.permutation(T)[:S]),
        "dst": striped(np.random.permutation(np.concatenate([np.arange(V), np.random.randint(0, V, S - V)]))),
    }


def reference(x_words, x_scales, w1, val0, offs, dst):
    xq = unpack_weight(x_words, x_scales)[:, unstriped(offs)]
    rew = -1.0 * (np.log(np.exp(mxq(f64(w1), 0, "e4m3").T @ xq) + 1.0))
    qa = rew + f64(val0)[:, unstriped(dst)]
    ea = np.exp(qa)
    va = np.log(ea.reshape(len(ea), -1, D).sum(axis=2))
    qb = rew + va[:, unstriped(dst)]
    eb = np.exp(qb)
    sb = eb.reshape(len(eb), -1, D).sum(axis=2)
    return np.log(sb)

@@ -1,0 +1,108 @@
+from contextlib import ExitStack
+
+import concourse.mybir as mybir
+
+K, T, S, N, V = 1024, 1024, 512, 128, 256
+FLOPS = 2 * K * S * N
+
+F32 = mybir.dt.float32
+BF16 = mybir.dt.bfloat16
+I32 = mybir.dt.int32
+U32 = mybir.dt.uint32
+U16 = mybir.dt.uint16
+U8 = mybir.dt.uint8
+FP8X4 = mybir.dt.float8_e4m3fn_x4
+ACT = mybir.ActivationFunctionType
+ALU = mybir.AluOpType
+
+P = 128
+PASSES = 2
+EDGE_CHUNKS = ((0, 256), (256, 384), (384, 512))
+DST_CHUNKS = ((0, 192), (192, 384), (384, 512))
+OUT_CHUNKS = ((0, 192), (192, 256))
+
+
+def tile_picked_ysoftvi_val_p_kernel(tc, x_words, x_scales, w1, val0, offs, dst, out):
+    nc = tc.nc
+    with ExitStack() as ctx:
+        sb = ctx.enter_context(tc.tile_pool(name="sb", bufs=1))
+        ps = ctx.enter_context(tc.psum_pool(name="ps", bufs=1))
+
+        offs_t = sb.tile([P, S // 16], U16, name="offs_t")
+        dst_t = sb.tile([P, S // 16], U16, name="dst_t")
+        scale_tab = sb.tile([P, T], U8, name="scale_tab", align_bytes=64)
+        word_tab = [sb.tile([P, T], U32, name=f"word_tab{o}", align_bytes=64) for o in range(PASSES)]
+        w_raw = sb.tile([P, PASSES, 4 * N], F32, name="w_raw", align_bytes=64)
+        val_t = sb.tile([P, V], F32, name="val_t", align_bytes=64)
+
+        nc.vector.memset(scale_tab[:].bitcast(I32), 0)
+        nc.sync.dma_start(offs_t[:], offs)
+        nc.sync.dma_start(out=val_t[:], in_=val0)
+        nc.sync.dma_start(dst_t[:], dst)
+        for q in range(4):
+            queue = nc.sync if q < 2 else nc.scalar
+            queue.dma_start(out=scale_tab[32 * q : 32 * q + 8, :].bitcast(I32), in_=x_scales[:, 4 * q : 4 * q + 4, :].bitcast(I32))
+        nc.sync.dma_start(out=word_tab[0][:].bitcast(I32), in_=x_words[0].rearrange("p n t -> p (n t)").bitcast(I32))
+        nc.sync.dma_start(out=w_raw[:], in_=w1.rearrange("(o p t) n -> p o (t n)", o=PASSES, t=4))
+        nc.sync.dma_start(out=word_tab[1][:].bitcast(I32), in_=x_words[1].rearrange("p n t -> p (n t)").bitcast(I32))
+
+        exp_val = sb.tile([P, V], F32, name="exp_val", align_bytes=64)
+        nc.scalar.activation(out=exp_val[:], in_=val_t[:], func=ACT.Exp)
+        exp_dst = sb.tile([P, S], F32, name="exp_dst", align_bytes=64)
+        for a, b in DST_CHUNKS:
+            nc.scalar.activation(out=exp_dst[:, a:b], in_=exp_val[:].indirect(dst_t[:, a // 16 : b // 16]), func=ACT.Copy)
+
+        x_scale = sb.tile([P, S], U8, name="x_scale", align_bytes=64)
+        nc.vector.tensor_copy(out=x_scale[:], in_=scale_tab[:].indirect(offs_t[:]))
+
+        x_code0 = sb.tile([P, S], U32, name="x_code0", align_bytes=64)
+        nc.vector.tensor_copy(out=x_code0[:], in_=word_tab[0][:].indirect(offs_t[:]))
+
+        w_bf = sb.tile([P, PASSES, N, 4], BF16, name="w_bf", tag="reuse", align_bytes=64)
+        for o, copy in enumerate((nc.vector.tensor_copy, nc.scalar.copy)):
+            copy(
+                out=w_bf[:, o].rearrange("p (c i) t -> p c t i", i=4),
+                in_=w_raw[:, o].rearrange("p (t c i) -> p c t i", t=4, i=4),
+            )
+        w_code = sb.tile([P, PASSES * N], U32, name="w_code", align_bytes=64)
+        w_scale = sb.tile([P, PASSES * N], U8, name="w_scale", align_bytes=64)
+        nc.vector.quantize_mx(out=w_code[:].bitcast(FP8X4), scales=w_scale[:], in_=w_bf[:].rearrange("p o n t -> p (o n t)"))
+
+        keep = sb.tile([P, S], F32, name="keep", align_bytes=64)
+        ea = sb.tile([P, S], F32, name="ea", align_bytes=64)
+        sa = sb.tile([P, V], F32, name="sa", align_bytes=64)
+        z = [ps.tile([P, b - a], F32, name=f"z{c}") for c, (a, b) in enumerate(EDGE_CHUNKS)]
+
+        def product_pass(o, c, codes):
+            a, b = EDGE_CHUNKS[c]
+            nc.tensor.matmul_mx(
+                out=z[c][:],
+                lhsT=w_code[:, o * N : (o + 1) * N].bitcast(FP8X4),
+                lhsT_scale=w_scale[:, o * N : (o + 1) * N],
+                rhs=codes.bitcast(FP8X4),
+                rhs_scale=x_scale[4 * o : P, a:b],
+                start=(o == 0),
+                stop=(o == PASSES - 1),
+            )
+
+        for c, (a, b) in enumerate(EDGE_CHUNKS):
+            product_pass(0, c, x_code0[:, a:b])
+        for c, (a, b) in enumerate(EDGE_CHUNKS):
+            x_code1 = sb.tile([P, b - a], U32, name=f"x_code1_{c}", tag="reuse" if c == 0 else f"x_code1_{c}", align_bytes=64)
+            nc.vector.tensor_copy(out=x_code1[:], in_=word_tab[1][:].indirect(offs_t[:, a // 16 : b // 16]))
+            product_pass(1, c, x_code1[:])
+            nc.scalar.activation(out=keep[:, a:b], in_=z[c][:], func=ACT.Sigmoid, scale=-1.0)
+        for a, b in EDGE_CHUNKS:
+            nc.vector.tensor_tensor(out=ea[:, a:b], in0=keep[:, a:b], in1=exp_dst[:, a:b], op=ALU.mult)
+        for a, b in EDGE_CHUNKS:
+            nc.vector.tensor_tensor(out=sa[:, a // 2 : b // 2], in0=ea[:, a:b:2], in1=ea[:, a + 1 : b : 2], op=ALU.add)
+
+        eb = sb.tile([P, S], F32, name="eb", align_bytes=64)
+        sums = sb.tile([P, V], F32, name="sums", align_bytes=64)
+        res = sb.tile([P, V], F32, name="res", align_bytes=64)
+        for a, b in DST_CHUNKS:
+            nc.vector.tensor_tensor(out=eb[:, a:b], in0=sa[:].indirect(dst_t[:, a // 16 : b // 16]), in1=keep[:, a:b], op=ALU.mult)
+        for a, b in OUT_CHUNKS:
+            nc.vector.tensor_tensor(out=sums[:, a:b], in0=eb[:, 2 * a : 2 * b : 2], in1=eb[:, 2 * a + 1 : 2 * b : 2], op=ALU.add)
+            nc.scalar.activation(out=res[:, a:b], in_=sums[:, a:b], func=ACT.Ln)
+            nc.sync.dma_start(out=out[:, a:b], in_=res[:, a:b])

@@ -32,7 +32,7 @@ def tile_picked_ysoftvi_val_p_kernel(tc, x_words, x_scales, w1, val0, offs, dst,
         dst_t = sb.tile([P, S // 16], U16, name="dst_t")
         scale_tab = sb.tile([P, T], U8, name="scale_tab", align_bytes=64)
         word_tab = [sb.tile([P, T], U32, name=f"word_tab{o}", align_bytes=64) for o in range(PASSES)]
-        w_raw = sb.tile([P, PASSES, 4 * N], F32, name="w_raw", align_bytes=64)
+        w_raw = sb.tile([P, PASSES, 4 * N], F32, name="w_raw", tag="w_raw", align_bytes=64)
         val_t = sb.tile([P, V], F32, name="val_t", align_bytes=64)
 
         nc.vector.memset(scale_tab[:].bitcast(I32), 0)
@@ -42,31 +42,37 @@ def tile_picked_ysoftvi_val_p_kernel(tc, x_words, x_scales, w1, val0, offs, dst,
         for q in range(4):
             queue = nc.sync if q < 2 else nc.scalar
             queue.dma_start(out=scale_tab[32 * q : 32 * q + 8, :].bitcast(I32), in_=x_scales[:, 4 * q : 4 * q + 4, :].bitcast(I32))
-        nc.sync.dma_start(out=word_tab[0][:].bitcast(I32), in_=x_words[0].rearrange("p n t -> p (n t)").bitcast(I32))
         nc.sync.dma_start(out=w_raw[:], in_=w1.rearrange("(o p t) n -> p o (t n)", o=PASSES, t=4))
-        nc.sync.dma_start(out=word_tab[1][:].bitcast(I32), in_=x_words[1].rearrange("p n t -> p (n t)").bitcast(I32))
+        for o in range(PASSES):
+            nc.sync.dma_start(out=word_tab[o][:].bitcast(I32), in_=x_words[o].rearrange("p n t -> p (n t)").bitcast(I32))
 
         exp_val = sb.tile([P, V], F32, name="exp_val", align_bytes=64)
         nc.scalar.activation(out=exp_val[:], in_=val_t[:], func=ACT.Exp)
-        exp_dst = sb.tile([P, S], F32, name="exp_dst", align_bytes=64)
-        for a, b in DST_CHUNKS:
-            nc.scalar.activation(out=exp_dst[:, a:b], in_=exp_val[:].indirect(dst_t[:, a // 16 : b // 16]), func=ACT.Copy)
+        head = DST_CHUNKS[0][1]
+        exp_head = sb.tile([P, head], F32, name="exp_head", align_bytes=64)
+        nc.scalar.activation(out=exp_head[:], in_=exp_val[:].indirect(dst_t[:, 0 : head // 16]), func=ACT.Copy)
 
         x_scale = sb.tile([P, S], U8, name="x_scale", align_bytes=64)
         nc.vector.tensor_copy(out=x_scale[:], in_=scale_tab[:].indirect(offs_t[:]))
 
-        x_code0 = sb.tile([P, S], U32, name="x_code0", align_bytes=64)
-        nc.vector.tensor_copy(out=x_code0[:], in_=word_tab[0][:].indirect(offs_t[:]))
-
-        w_bf = sb.tile([P, PASSES, N, 4], BF16, name="w_bf", tag="reuse", align_bytes=64)
+        w_bf = sb.tile([P, PASSES, N, 4], BF16, name="w_bf", align_bytes=64)
         for o, copy in enumerate((nc.vector.tensor_copy, nc.scalar.copy)):
             copy(
                 out=w_bf[:, o].rearrange("p (c i) t -> p c t i", i=4),
                 in_=w_raw[:, o].rearrange("p (t c i) -> p c t i", t=4, i=4),
             )
+        exp_rest = sb.tile([P, S - head], F32, name="exp_rest", tag="w_raw", align_bytes=64)
+        for a, b in DST_CHUNKS[1:]:
+            nc.scalar.activation(out=exp_rest[:, a - head : b - head], in_=exp_val[:].indirect(dst_t[:, a // 16 : b // 16]), func=ACT.Copy)
         w_code = sb.tile([P, PASSES * N], U32, name="w_code", align_bytes=64)
         w_scale = sb.tile([P, PASSES * N], U8, name="w_scale", align_bytes=64)
-        nc.vector.quantize_mx(out=w_code[:].bitcast(FP8X4), scales=w_scale[:], in_=w_bf[:].rearrange("p o n t -> p (o n t)"))
+        for o in range(PASSES):
+            cols = slice(o * N, (o + 1) * N)
+            nc.vector.quantize_mx(out=w_code[:, cols].bitcast(FP8X4), scales=w_scale[:, cols], in_=w_bf[:, o].rearrange("p n t -> p (n t)"))
+
+        x_code0 = sb.tile([P, S], U32, name="x_code0", align_bytes=64)
+        for a, b in ((0, 256), (256, 512)):
+            nc.vector.tensor_copy(out=x_code0[:, a:b], in_=word_tab[0][:].indirect(offs_t[:, a // 16 : b // 16]))
 
         keep = sb.tile([P, S], F32, name="keep", align_bytes=64)
         ea = sb.tile([P, S], F32, name="ea", align_bytes=64)
@@ -88,13 +94,14 @@ def tile_picked_ysoftvi_val_p_kernel(tc, x_words, x_scales, w1, val0, offs, dst,
         for c, (a, b) in enumerate(EDGE_CHUNKS):
             product_pass(0, c, x_code0[:, a:b])
         for c, (a, b) in enumerate(EDGE_CHUNKS):
-            x_code1 = sb.tile([P, b - a], U32, name=f"x_code1_{c}", tag="reuse" if c == 0 else f"x_code1_{c}", align_bytes=64)
+            x_code1 = sb.tile([P, b - a], U32, name=f"x_code1_{c}", align_bytes=64)
             nc.vector.tensor_copy(out=x_code1[:], in_=word_tab[1][:].indirect(offs_t[:, a // 16 : b // 16]))
             product_pass(1, c, x_code1[:])
             nc.scalar.activation(out=keep[:, a:b], in_=z[c][:], func=ACT.Sigmoid, scale=-1.0)
-        for a, b in EDGE_CHUNKS:
-            nc.vector.tensor_tensor(out=ea[:, a:b], in0=keep[:, a:b], in1=exp_dst[:, a:b], op=ALU.mult)
-        for a, b in EDGE_CHUNKS:
+        for a, b in DST_CHUNKS:
+            exp_dst = exp_head[:] if a == 0 else exp_rest[:, a - head : b - head]
+            nc.vector.tensor_tensor(out=ea[:, a:b], in0=keep[:, a:b], in1=exp_dst, op=ALU.mult)
+        for a, b in DST_CHUNKS:
             nc.vector.tensor_tensor(out=sa[:, a // 2 : b // 2], in0=ea[:, a:b:2], in1=ea[:, a + 1 : b : 2], op=ALU.add)
 
         eb = sb.tile([P, S], F32, name="eb", align_bytes=64)

from contextlib import ExitStack

import concourse.mybir as mybir

K, T, S, N, V = 1024, 1024, 512, 128, 256
FLOPS = 2 * K * S * N

F32 = mybir.dt.float32
BF16 = mybir.dt.bfloat16
I32 = mybir.dt.int32
U32 = mybir.dt.uint32
U16 = mybir.dt.uint16
U8 = mybir.dt.uint8
FP8X4 = mybir.dt.float8_e4m3fn_x4
ACT = mybir.ActivationFunctionType
ALU = mybir.AluOpType

P = 128
PASSES = 2
EDGE_CHUNKS = ((0, 256), (256, 384), (384, 512))
DST_CHUNKS = ((0, 192), (192, 384), (384, 512))
OUT_CHUNKS = ((0, 192), (192, 256))


def tile_picked_ysoftvi_val_p_kernel(tc, x_words, x_scales, w1, val0, offs, dst, out):
    nc = tc.nc
    with ExitStack() as ctx:
        sb = ctx.enter_context(tc.tile_pool(name="sb", bufs=1))
        ps = ctx.enter_context(tc.psum_pool(name="ps", bufs=1))

        offs_t = sb.tile([P, S // 16], U16, name="offs_t")
        dst_t = sb.tile([P, S // 16], U16, name="dst_t")
        scale_tab = sb.tile([P, T], U8, name="scale_tab", align_bytes=64)
        word_tab = [sb.tile([P, T], U32, name=f"word_tab{o}", align_bytes=64) for o in range(PASSES)]
        w_raw = sb.tile([P, PASSES, 4 * N], F32, name="w_raw", tag="w_raw", align_bytes=64)
        val_t = sb.tile([P, V], F32, name="val_t", align_bytes=64)

        nc.vector.memset(scale_tab[:].bitcast(I32), 0)
        nc.sync.dma_start(offs_t[:], offs)
        nc.sync.dma_start(out=val_t[:], in_=val0)
        nc.sync.dma_start(dst_t[:], dst)
        for q in range(4):
            queue = nc.sync if q < 2 else nc.scalar
            queue.dma_start(out=scale_tab[32 * q : 32 * q + 8, :].bitcast(I32), in_=x_scales[:, 4 * q : 4 * q + 4, :].bitcast(I32))
        nc.sync.dma_start(out=w_raw[:], in_=w1.rearrange("(o p t) n -> p o (t n)", o=PASSES, t=4))
        for o in range(PASSES):
            nc.sync.dma_start(out=word_tab[o][:].bitcast(I32), in_=x_words[o].rearrange("p n t -> p (n t)").bitcast(I32))

        exp_val = sb.tile([P, V], F32, name="exp_val", align_bytes=64)
        nc.scalar.activation(out=exp_val[:], in_=val_t[:], func=ACT.Exp)
        head = DST_CHUNKS[0][1]
        exp_head = sb.tile([P, head], F32, name="exp_head", align_bytes=64)
        nc.scalar.activation(out=exp_head[:], in_=exp_val[:].indirect(dst_t[:, 0 : head // 16]), func=ACT.Copy)

        x_scale = sb.tile([P, S], U8, name="x_scale", align_bytes=64)
        nc.vector.tensor_copy(out=x_scale[:], in_=scale_tab[:].indirect(offs_t[:]))

        w_bf = sb.tile([P, PASSES, N, 4], BF16, name="w_bf", align_bytes=64)
        for o, copy in enumerate((nc.vector.tensor_copy, nc.scalar.copy)):
            copy(
                out=w_bf[:, o].rearrange("p (c i) t -> p c t i", i=4),
                in_=w_raw[:, o].rearrange("p (t c i) -> p c t i", t=4, i=4),
            )
        exp_rest = sb.tile([P, S - head], F32, name="exp_rest", tag="w_raw", align_bytes=64)
        for a, b in DST_CHUNKS[1:]:
            nc.scalar.activation(out=exp_rest[:, a - head : b - head], in_=exp_val[:].indirect(dst_t[:, a // 16 : b // 16]), func=ACT.Copy)
        w_code = sb.tile([P, PASSES * N], U32, name="w_code", align_bytes=64)
        w_scale = sb.tile([P, PASSES * N], U8, name="w_scale", align_bytes=64)
        for o in range(PASSES):
            cols = slice(o * N, (o + 1) * N)
            nc.vector.quantize_mx(out=w_code[:, cols].bitcast(FP8X4), scales=w_scale[:, cols], in_=w_bf[:, o].rearrange("p n t -> p (n t)"))

        x_code0 = sb.tile([P, S], U32, name="x_code0", align_bytes=64)
        for a, b in ((0, 256), (256, 512)):
            nc.vector.tensor_copy(out=x_code0[:, a:b], in_=word_tab[0][:].indirect(offs_t[:, a // 16 : b // 16]))

        keep = sb.tile([P, S], F32, name="keep", align_bytes=64)
        ea = sb.tile([P, S], F32, name="ea", align_bytes=64)
        sa = sb.tile([P, V], F32, name="sa", align_bytes=64)
        z = [ps.tile([P, b - a], F32, name=f"z{c}") for c, (a, b) in enumerate(EDGE_CHUNKS)]

        def product_pass(o, c, codes):
            a, b = EDGE_CHUNKS[c]
            nc.tensor.matmul_mx(
                out=z[c][:],
                lhsT=w_code[:, o * N : (o + 1) * N].bitcast(FP8X4),
                lhsT_scale=w_scale[:, o * N : (o + 1) * N],
                rhs=codes.bitcast(FP8X4),
                rhs_scale=x_scale[4 * o : P, a:b],
                start=(o == 0),
                stop=(o == PASSES - 1),
            )

        for c, (a, b) in enumerate(EDGE_CHUNKS):
            product_pass(0, c, x_code0[:, a:b])
        for c, (a, b) in enumerate(EDGE_CHUNKS):
            x_code1 = sb.tile([P, b - a], U32, name=f"x_code1_{c}", align_bytes=64)
            nc.vector.tensor_copy(out=x_code1[:], in_=word_tab[1][:].indirect(offs_t[:, a // 16 : b // 16]))
            product_pass(1, c, x_code1[:])
            nc.scalar.activation(out=keep[:, a:b], in_=z[c][:], func=ACT.Sigmoid, scale=-1.0)
        for a, b in DST_CHUNKS:
            exp_dst = exp_head[:] if a == 0 else exp_rest[:, a - head : b - head]
            nc.vector.tensor_tensor(out=ea[:, a:b], in0=keep[:, a:b], in1=exp_dst, op=ALU.mult)
        for a, b in DST_CHUNKS:
            nc.vector.tensor_tensor(out=sa[:, a // 2 : b // 2], in0=ea[:, a:b:2], in1=ea[:, a + 1 : b : 2], op=ALU.add)

        eb = sb.tile([P, S], F32, name="eb", align_bytes=64)
        sums = sb.tile([P, V], F32, name="sums", align_bytes=64)
        res = sb.tile([P, V], F32, name="res", align_bytes=64)
        for a, b in DST_CHUNKS:
            nc.vector.tensor_tensor(out=eb[:, a:b], in0=sa[:].indirect(dst_t[:, a // 16 : b // 16]), in1=keep[:, a:b], op=ALU.mult)
        for a, b in OUT_CHUNKS:
            nc.vector.tensor_tensor(out=sums[:, a:b], in0=eb[:, 2 * a : 2 * b : 2], in1=eb[:, 2 * a + 1 : 2 * b : 2], op=ALU.add)
            nc.scalar.activation(out=res[:, a:b], in_=sums[:, a:b], func=ACT.Ln)
            nc.sync.dma_start(out=out[:, a:b], in_=res[:, a:b])
